import numpy as np
import ml_dtypes


def mxq(x, axis, fmt="e4m3"):
    dtype, down = {"e4m3": (ml_dtypes.float8_e4m3fn, 7), "e5m2": (ml_dtypes.float8_e5m2, 14)}[fmt]
    v = np.moveaxis(np.asarray(x, np.float32).astype(ml_dtypes.bfloat16).astype(np.float64), axis, -1)
    blocks = v.reshape(v.shape[:-1] + (-1, 32))
    amax = np.abs(blocks).max(-1, keepdims=True)
    byte = np.maximum(np.where(amax > 0, np.frexp(amax)[1] - 1 + 127, 0) - down, 1)
    scale = np.exp2(byte - 127.0)
    codes = (blocks / scale).astype(np.float32).astype(dtype).astype(np.float64)
    return np.moveaxis((codes * scale).reshape(v.shape), -1, axis)


WIDE = False


def mx_kscale(k):
    if not WIDE:
        return np.ones(k)
    levels = np.array([10, -10, 5, -5, 0])
    if k % 512:
        return np.exp2(np.random.permutation(np.resize(levels, k // 32))).repeat(32)
    a = np.empty((k // 512, 16))
    for p in range(k // 512):
        a[p, :8] = np.random.permutation(np.resize(levels, 8))
        for g in range(8):
            far = levels[np.abs(levels - a[p, g]) >= 10]
            a[p, g + 8] = far[np.random.randint(len(far))]
    return np.exp2(a.ravel()).repeat(32)


def f64(x):
    return np.asarray(x).astype(np.float64)


def striped(idx):
    return np.tile(idx.reshape(-1, 16).T, (8, 1)).astype(np.uint16)


def unstriped(offs):
    return offs[:16].T.reshape(-1).astype(np.int64)


E2M1 = np.array([0.0, 0.5, 1.0, 1.5, 2.0, 3.0, 4.0, 6.0, -0.0, -0.5, -1.0, -1.5, -2.0, -3.0, -4.0, -6.0])


def pack_weight(w, fmt):
    k, n = w.shape
    w = f64(np.asarray(w, np.float32).astype(ml_dtypes.bfloat16)).reshape(k // 32, 32, n)
    amax = np.abs(w).max(1)
    if fmt == "e4m3":
        byte = np.frexp(amax)[1] - 1 + 127 - 7
    else:
        mant, ex = np.frexp(amax / 6.0)
        byte = np.where(mant > 0.5, ex, ex - 1) + 127
    byte = np.clip(np.where(amax > 0, byte, 1), 1, 254)
    scaled = (w * np.exp2(127.0 - byte)[:, None, :]).reshape(k, n).astype(np.float32)
    by_word = np.ascontiguousarray(scaled.reshape(k // 512, 128, 4, n).transpose(0, 1, 3, 2))
    if fmt == "e4m3":
        words = by_word.astype(ml_dtypes.float8_e4m3fn).view(np.uint8)
    else:
        c = by_word.astype(ml_dtypes.float4_e2m1fn).view(np.uint8) & 0xF
        words = (c[..., 0::2] | (c[..., 1::2] << 4)).reshape(k // 512, 128, 2 * n)
    return np.ascontiguousarray(words), np.ascontiguousarray(byte.astype(np.uint8).reshape(k // 512, 16, n))


def unpack_weight(words, scales, fmt):
    g, _, n = scales.shape
    words = np.ascontiguousarray(words).reshape(g, 128, n, -1)
    if fmt == "e4m3":
        vals = words.view(ml_dtypes.float8_e4m3fn).astype(np.float64)
    else:
        nib = np.empty((g, 128, n, 4), np.uint8)
        nib[..., 0::2] = words & 0xF
        nib[..., 1::2] = words >> 4
        vals = E2M1[nib]
    vals = vals * np.repeat(np.exp2(scales.astype(np.float64) - 127.0), 8, axis=1)[..., None]
    return vals.transpose(0, 1, 3, 2).reshape(g * 512, n)


def gelu(v):
    return 0.5 * v * (1.0 + np.tanh(np.sqrt(2.0 / np.pi) * (v + 0.044715 * v**3)))


def striped8(idx):
    return np.concatenate([v.reshape(-1, 16).T for v in idx]).astype(np.uint16)


def unstriped8(offs):
    return np.stack([offs[16 * g:16 * g + 16].T.reshape(-1) for g in range(8)]).astype(np.int64)


def heads(h, wgt, idx8):
    r = np.arange(h.shape[0])
    return wgt[r // 4 % 128] * h[r[:, None], idx8[r % 512 // 64]]


def put_heads(h, wgs, idx8, t2):
    r = np.arange(h.shape[0])
    page = np.zeros((h.shape[0], t2))
    page[r[:, None], idx8[r % 512 // 64]] = wgs[r // 4 % 128] * h
    return page


K, T, S, H, T2, P, N = 1536, 2048, 512, 1024, 1024, 512, 512

def setup_inputs():
    n = np.random.standard_normal
    s = mx_kscale(K)[:, None]
    u = mx_kscale(H)[:, None]
    d = {}
    d["tab_words"], d["tab_scales"] = pack_weight(n((K, T)) * s, "e4m3")
    d["offs"] = striped(np.random.permutation(T)[:S])
    d["w1"] = (2.0 * n((K, H)) / K**0.5 / s * u.T).astype(np.float32)
    d["unit"] = (np.exp(0.5 * n(H)) * u[:, 0]**2).astype(np.float32)
    d["offs2"] = striped8(np.stack([np.random.permutation(T2)[:S] for _ in range(8)]))
    d["wgs"] = np.repeat(np.random.uniform(0.5, 2.0, (8, S)), 16, axis=0).astype(np.float32)
    d["offs3"] = striped8(np.stack([np.random.permutation(T2)[:P] for _ in range(8)]))
    d["wgt"] = np.repeat(np.random.uniform(0.5, 2.0, (8, P)), 16, axis=0).astype(np.float32)
    d["gust"] = ((1.2 + 1.5 * n((H, P))) * u).astype(np.float32)
    d["wa"] = (0.6 * n((H, N)) / H**0.5 / u).astype(np.float32)
    d["wb_words"], d["wb_scales"] = pack_weight(0.35 * n((H, N)) / H**0.5 / u, "e2m1")
    d["wd_words"], d["wd_scales"] = pack_weight(0.3 * n((H, N)) / H**0.5 / u, "e4m3")
    return d

def reference(tab_words, tab_scales, offs, w1, unit, offs2, wgs, offs3, wgt, gust, wa, wb_words, wb_scales, wd_words, wd_scales):
    v = unpack_weight(tab_words, tab_scales, "e4m3")[:, unstriped(offs)]
    p = mxq(f64(w1), 0, "e4m3").T @ v
    h = np.sqrt(f64(unit)[:, None] + np.square(p))
    page = put_heads(h, f64(wgs), unstriped8(offs2), T2)
    x = heads(page, f64(wgt), unstriped8(offs3))
    z = mxq(x - f64(gust), 0, "e4m3")
    y1 = mxq(f64(wa), 0, "e4m3").T @ z
    y2 = unpack_weight(wb_words, wb_scales, "e2m1").T @ z
    y3 = unpack_weight(wd_words, wd_scales, "e4m3").T @ z
    return np.maximum(np.tanh(y1), y2) + y3

@@ -1,0 +1,267 @@
+from contextlib import ExitStack
+
+import concourse.mybir as mybir
+
+K, T, S, H, T2, M, N = 1536, 2048, 512, 1024, 1024, 512, 512
+FLOPS = 2 * K * H * S + 3 * 2 * H * N * M
+
+F32 = mybir.dt.float32
+BF16 = mybir.dt.bfloat16
+I32 = mybir.dt.int32
+U32 = mybir.dt.uint32
+U16 = mybir.dt.uint16
+U8 = mybir.dt.uint8
+FP8X4 = mybir.dt.float8_e4m3fn_x4
+FP4X4 = mybir.dt.float4_e2m1fn_x4
+ACT = mybir.ActivationFunctionType
+ALU = mybir.AluOpType
+
+P = 128
+PASS = 512
+KP = K // PASS
+HP = H // PASS
+CH = 128
+NCH = M // CH
+NT = N // P
+
+
+def tile_list_slew_load_features_kernel(
+    tc, tab_words, tab_scales, offs, w1, unit, offs2, wgs, offs3, wgt, gust, wa,
+    wb_words, wb_scales, wd_words, wd_scales, out,
+):
+    nc = tc.nc
+    with ExitStack() as ctx:
+        lists = ctx.enter_context(tc.tile_pool(name="lists", bufs=1))
+        keep = ctx.enter_context(tc.tile_pool(name="keep", bufs=1))
+        psum = ctx.enter_context(tc.psum_pool(name="psum", bufs=1))
+
+        def sb(shape, dtype, name, tag=None, bufs=1):
+            return keep.tile(shape, dtype, name=name, tag=tag or name, bufs=bufs, align_bytes=64)
+
+        def bank(k, name):
+            return psum.tile([P, 512], F32, name=name, tag="bank%d" % k)
+
+        def load_rows(src, name):
+            raw = sb([P, 4, 512], F32, name, tag="raw", bufs=5)
+            nc.sync.dma_start(out=raw[:], in_=src.rearrange("(p j) c -> p j c", j=4))
+            return raw
+
+        def quantise(grouped, name):
+            width = grouped.shape[1] // 4
+            codes = sb([P, width], U32, name + "_codes")
+            scales = sb([P, width], U8, name + "_scales")
+            nc.vector.quantize_mx(out=codes[:].bitcast(FP8X4), scales=scales[:], in_=grouped[:])
+            return codes, scales
+
+        def interleave(src, name, tag, bufs):
+            width = src.shape[2]
+            grouped = sb([P, 4 * width], BF16, name, tag=tag, bufs=bufs)
+            nc.scalar.copy(
+                out=grouped[:].rearrange("p (a c j) -> p a j c", c=4, j=4),
+                in_=src[:].rearrange("p j (a c) -> p a j c", c=4),
+            )
+            return grouped
+
+        def deal_w1(raw, name, tag, bufs):
+            grouped = sb([P, 2048], BF16, name, tag=tag, bufs=bufs)
+            nc.scalar.copy(
+                out=grouped[:].rearrange("p (t m j) -> p m j t", t=4, j=4),
+                in_=raw[:].rearrange("p j (m t) -> p m j t", t=4),
+            )
+            return grouped
+
+        tab_sc = sb([P, T], U8, "tab_sc")
+        wb_sc = sb([P, HP, N], U8, "wb_sc")
+        wd_sc = sb([P, HP, N], U8, "wd_sc")
+        nc.vector.memset(tab_sc[:].bitcast(I32), 0)
+        for q in range(4):
+            nc.scalar.dma_start(
+                out=tab_sc[32 * q : 32 * q + 4 * KP, :].bitcast(I32),
+                in_=tab_scales[:, 4 * q : 4 * q + 4, :].bitcast(I32),
+            )
+        nc.gpsimd.memset(wb_sc[:].bitcast(I32), 0)
+        nc.gpsimd.memset(wd_sc[:].bitcast(I32), 0)
+        pages = []
+        for i in range(4):
+            page = sb([P, T2], F32, "page%d" % i)
+            nc.vector.memset(page[:], 0.0)
+            pages.append(page)
+
+        idx = lists.tile([P, S // 16], U16, name="idx")
+        idx2 = lists.tile([P, S // 16], U16, name="idx2")
+        idx3 = lists.tile([P, M // 16], U16, name="idx3")
+        nc.sync.dma_start(idx[:], offs)
+        tab = [sb([P, T], I32, "tab%d" % a) for a in range(KP)]
+
+        def load_tab(a):
+            nc.sync.dma_start(
+                out=tab[a][:], in_=tab_words[a].rearrange("p t i -> p (t i)").bitcast(I32)
+            )
+
+        def load_w1(a, b):
+            return load_rows(
+                w1[PASS * a : PASS * (a + 1), PASS * b : PASS * (b + 1)], "w1raw%d%d" % (a, b)
+            )
+
+        w1_raw = {}
+        w1_raw[0, 0] = load_w1(0, 0)
+        w1_raw[1, 0] = load_w1(1, 0)
+        load_tab(0)
+        w1_raw[2, 0] = load_w1(2, 0)
+        load_tab(1)
+        load_tab(2)
+        unit_sb = sb([P, HP, 4], F32, "unit_sb")
+        nc.sync.dma_start(out=unit_sb[:], in_=unit.rearrange("(b p i) -> p b i", b=HP, i=4))
+        nc.sync.dma_start(idx2[:], offs2)
+        wgs_sb = sb([P, S], F32, "wgs_sb", tag="slot_b")
+        nc.sync.dma_start(out=wgs_sb[:], in_=wgs)
+
+        w1_q = {}
+        for a in range(KP):
+            w1_q[a, 0] = quantise(deal_w1(w1_raw[a, 0], "w1g%d0" % a, "grp", 3), "w1q%d0" % a)
+        v_sc = sb([P, S], U8, "v_sc")
+        nc.vector.tensor_copy(v_sc[:], tab_sc[:].indirect(idx[:]))
+        v = [sb([P, S], U32, "v%d" % a) for a in range(KP)]
+        for a in range(KP - 1):
+            nc.vector.tensor_copy(v[a][:], tab[a][:].bitcast(U32).indirect(idx[:]))
+        half = S // 2
+        for lo in (0, half):
+            nc.vector.tensor_copy(
+                v[KP - 1][:, lo : lo + half],
+                tab[KP - 1][:].bitcast(U32).indirect(idx[:, lo // 16 : (lo + half) // 16]),
+            )
+
+        def p_pass(acc, a, b, i, lo, hi):
+            codes, scales = w1_q[a, b]
+            nc.tensor.matmul_mx(
+                out=acc[:, 0 : hi - lo],
+                lhsT=codes[:, P * i : P * (i + 1)].bitcast(FP8X4),
+                lhsT_scale=scales[:, P * i : P * (i + 1)],
+                rhs=v[a][:, lo:hi].bitcast(FP8X4),
+                rhs_scale=v_sc[4 * a : P, lo:hi],
+                start=(a == 0),
+                stop=(a == KP - 1),
+            )
+
+        def magnitude(acc, h, b, i, lo, hi):
+            sq = sb([P, S], F32, "sq%d%d%d" % (b, i, lo), tag="sq", bufs=2)
+            nc.scalar.activation(sq[:, 0 : hi - lo], acc[:, 0 : hi - lo], ACT.Square)
+            nc.scalar.activation(
+                h[:, lo:hi], sq[:, 0 : hi - lo], ACT.Sqrt, bias=unit_sb[:, b, i : i + 1]
+            )
+
+        def put(h, i, lo, hi):
+            nc.vector.tensor_tensor(
+                pages[i][:].indirect(idx2[:, lo // 16 : hi // 16]),
+                h[:, lo:hi], wgs_sb[:, lo:hi], ALU.mult,
+            )
+
+        pieces = [(0, 0, half), (0, half, S), (1, 0, S), (2, 0, S), (3, 0, S)]
+        accs = [bank(k, "p0_%d" % k) for k in range(len(pieces))]
+        for a in range(KP - 1):
+            for acc, (i, lo, hi) in zip(accs, pieces):
+                p_pass(acc, a, 0, i, lo, hi)
+        h0 = [sb([P, S], F32, "h0%d" % i) for i in range(4)]
+        for acc, (i, lo, hi) in zip(accs, pieces):
+            p_pass(acc, KP - 1, 0, i, lo, hi)
+            magnitude(acc, h0[i], 0, i, lo, hi)
+            put(h0[i], i, lo, hi)
+
+        for a in range(KP):
+            w1_raw[a, 1] = load_w1(a, 1)
+        nc.sync.dma_start(idx3[:], offs3)
+        wgt_sb = sb([P, M], F32, "wgt_sb")
+        nc.sync.dma_start(out=wgt_sb[:], in_=wgt)
+        gust_sb = [sb([P, 4, M], F32, "gust%d" % b) for b in range(HP)]
+
+        def load_gust(b):
+            nc.sync.dma_start(
+                out=gust_sb[b][:],
+                in_=gust[PASS * b : PASS * (b + 1), :].rearrange("(p i) m -> p i m", i=4),
+            )
+
+        load_gust(0)
+        wa_raw = [load_rows(wa[PASS * b : PASS * (b + 1), :], "waraw%d" % b) for b in range(HP)]
+        load_gust(1)
+        wd_w = sb([P, HP, N], I32, "wd_w")
+        nc.sync.dma_start(
+            out=wd_w[:], in_=wd_words.rearrange("a p c i -> p a (c i)").bitcast(I32)
+        )
+        wb_w = sb([P, HP, 2 * N], U8, "wb_w")
+        nc.sync.dma_start(
+            out=wb_w[:].bitcast(I32), in_=wb_words.rearrange("a p c -> p a c").bitcast(I32)
+        )
+        for plane, src in ((wd_sc, wd_scales), (wb_sc, wb_scales)):
+            for q in range(4):
+                nc.sync.dma_start(
+                    out=plane[32 * q : 32 * q + 4, :, :].bitcast(I32),
+                    in_=src[:, 4 * q : 4 * q + 4, :].rearrange("a r c -> r a c").bitcast(I32),
+                )
+
+        for a in range(KP):
+            last = a == KP - 1
+            grouped = deal_w1(w1_raw[a, 1], "w1g%d1" % a, "x0" if last else "grp", 1 if last else 3)
+            w1_q[a, 1] = quantise(grouped, "w1q%d1" % a)
+
+        def pick(dst, i, lo, hi):
+            nc.vector.tensor_tensor(
+                dst, pages[i][:].indirect(idx3[:, lo // 16 : hi // 16]), wgt_sb[:, lo:hi], ALU.mult
+            )
+
+        x0 = sb([P, 4, M], F32, "x0", tag="x0")
+        for i in range(4):
+            pick(x0[:, i, :], i, 0, M)
+        nc.vector.tensor_tensor(x0[:], x0[:], gust_sb[0][:], ALU.subtract)
+
+        h1 = [sb([P, S], F32, "h1%d" % i, tag="slot_a" if i == 3 else None) for i in range(4)]
+        for i in range(4):
+            acc = bank((5 + i) % 8, "p1_%d" % i)
+            for a in range(KP):
+                p_pass(acc, a, 1, i, 0, S)
+            magnitude(acc, h1[i], 1, i, 0, S)
+            put(h1[i], i, 0, S)
+
+        z0 = quantise(interleave(x0, "z0g", "grp", 3), "z0")
+        wa_q = [
+            quantise(interleave(wa_raw[b], "wag%d" % b, "grp", 3), "waq%d" % b) for b in range(HP)
+        ]
+
+        def weights(kind, b, nt):
+            cols = slice(P * nt, P * (nt + 1))
+            if kind == 0:
+                return wa_q[b][0][:, cols].bitcast(FP8X4), wa_q[b][1][:, cols]
+            if kind == 1:
+                return wb_w[:, b, 2 * P * nt : 2 * P * (nt + 1)].bitcast(FP4X4), wb_sc[:, b, cols]
+            return wd_w[:, b, cols].bitcast(FP8X4), wd_sc[:, b, cols]
+
+        def y_passes(acc, kind, b, z_codes, z_scales):
+            for nt in range(NT):
+                w_codes, w_scales = weights(kind, b, nt)
+                nc.tensor.matmul_mx(
+                    out=acc[:, CH * nt : CH * (nt + 1)],
+                    lhsT=w_codes, lhsT_scale=w_scales,
+                    rhs=z_codes.bitcast(FP8X4), rhs_scale=z_scales,
+                    start=(b == 0 and nt == 0),
+                    stop=(b == HP - 1 and nt == NT - 1),
+                )
+
+        y_banks = [(1, 2, 3), (4, 5, 6), (7, 0, 1), (4, 2, 3)]
+        out_view = out.rearrange("(nt p) m -> p nt m", p=P)
+        for c in range(NCH):
+            cols = slice(CH * c, CH * (c + 1))
+            x = sb([P, 4, CH], F32, "x1%d" % c, tag="slot_b" if c % 2 else "slot_a")
+            for i in range(4):
+                pick(x[:, i, :], i, CH * c, CH * (c + 1))
+            nc.vector.tensor_tensor(x[:], x[:], gust_sb[1][:, :, cols], ALU.subtract)
+            z1 = quantise(interleave(x, "z1g%d" % c, "z1g", 2), "z1%d" % c)
+            y = [bank(y_banks[c][kind], "y%d%d" % (kind, c)) for kind in range(3)]
+            for kind in range(3):
+                y_passes(y[kind], kind, 0, z0[0][:, cols], z0[1][:, cols])
+            for kind in range(3):
+                y_passes(y[kind], kind, 1, z1[0][:], z1[1][:])
+            top = sb([P, N], F32, "top%d" % c, tag="top", bufs=2)
+            nc.scalar.activation(top[:], y[0][:], ACT.Tanh)
+            nc.vector.tensor_tensor(top[:], y[1][:], top[:], ALU.max)
+            res = sb([P, NT, CH], F32, "res%d" % c, tag="res", bufs=3)
+            nc.vector.tensor_tensor(res[:].rearrange("p t m -> p (t m)"), y[2][:], top[:], ALU.add)
+            nc.sync.dma_start(out=out_view[:, :, cols], in_=res[:])

@@ -1,6 +1,7 @@
 from contextlib import ExitStack
 
 import concourse.mybir as mybir
+from concourse.masks import make_identity
 
 K, T, S, H, T2, M, N = 1536, 2048, 512, 1024, 1024, 512, 512
 FLOPS = 2 * K * H * S + 3 * 2 * H * N * M
@@ -42,7 +43,7 @@ def tile_list_slew_load_features_kernel(
             return psum.tile([P, 512], F32, name=name, tag="bank%d" % k)
 
         def load_rows(src, name):
-            raw = sb([P, 4, 512], F32, name, tag="raw", bufs=5)
+            raw = sb([P, 4, 512], F32, name, tag="raw", bufs=3)
             nc.sync.dma_start(out=raw[:], in_=src.rearrange("(p j) c -> p j c", j=4))
             return raw
 
@@ -73,12 +74,18 @@ def tile_list_slew_load_features_kernel(
         tab_sc = sb([P, T], U8, "tab_sc")
         wb_sc = sb([P, HP, N], U8, "wb_sc")
         wd_sc = sb([P, HP, N], U8, "wd_sc")
-        nc.vector.memset(tab_sc[:].bitcast(I32), 0)
+        nc.gpsimd.memset(tab_sc[:].bitcast(I32), 0)
         for q in range(4):
             nc.scalar.dma_start(
                 out=tab_sc[32 * q : 32 * q + 4 * KP, :].bitcast(I32),
                 in_=tab_scales[:, 4 * q : 4 * q + 4, :].bitcast(I32),
             )
+        warm = sb([P, 8], F32, "warm")
+        nc.gpsimd.memset(warm[:], 1.0)
+        warm_out = sb([P, 8], F32, "warm_out")
+        nc.scalar.activation(warm_out[:], warm[:], ACT.Sqrt)
+        ident = sb([P, P], F32, "ident")
+        make_identity(nc, ident[:])
         nc.gpsimd.memset(wb_sc[:].bitcast(I32), 0)
         nc.gpsimd.memset(wd_sc[:].bitcast(I32), 0)
         pages = []
@@ -91,6 +98,10 @@ def tile_list_slew_load_features_kernel(
         idx2 = lists.tile([P, S // 16], U16, name="idx2")
         idx3 = lists.tile([P, M // 16], U16, name="idx3")
         nc.sync.dma_start(idx[:], offs)
+        nc.sync.dma_start(idx2[:], offs2)
+        nc.sync.dma_start(idx3[:], offs3)
+        unit_sb = sb([P, HP, 4], F32, "unit_sb")
+        nc.sync.dma_start(out=unit_sb[:], in_=unit.rearrange("(b p i) -> p b i", b=HP, i=4))
         tab = [sb([P, T], I32, "tab%d" % a) for a in range(KP)]
 
         def load_tab(a):
@@ -110,9 +121,6 @@ def tile_list_slew_load_features_kernel(
         w1_raw[2, 0] = load_w1(2, 0)
         load_tab(1)
         load_tab(2)
-        unit_sb = sb([P, HP, 4], F32, "unit_sb")
-        nc.sync.dma_start(out=unit_sb[:], in_=unit.rearrange("(b p i) -> p b i", b=HP, i=4))
-        nc.sync.dma_start(idx2[:], offs2)
         wgs_sb = sb([P, S], F32, "wgs_sb", tag="slot_b")
         nc.sync.dma_start(out=wgs_sb[:], in_=wgs)
 
@@ -143,8 +151,8 @@ def tile_list_slew_load_features_kernel(
                 stop=(a == KP - 1),
             )
 
-        def magnitude(acc, h, b, i, lo, hi):
-            sq = sb([P, S], F32, "sq%d%d%d" % (b, i, lo), tag="sq", bufs=2)
+        def magnitude(acc, h, b, i, lo, hi, slot):
+            sq = sb([P, S], F32, "sq%d%d%d" % (b, i, lo), tag=slot)
             nc.scalar.activation(sq[:, 0 : hi - lo], acc[:, 0 : hi - lo], ACT.Square)
             nc.scalar.activation(
                 h[:, lo:hi], sq[:, 0 : hi - lo], ACT.Sqrt, bias=unit_sb[:, b, i : i + 1]
@@ -159,20 +167,23 @@ def tile_list_slew_load_features_kernel(
         pieces = [(0, 0, half), (0, half, S), (1, 0, S), (2, 0, S), (3, 0, S)]
         accs = [bank(k, "p0_%d" % k) for k in range(len(pieces))]
         for a in range(KP - 1):
-            for acc, (i, lo, hi) in zip(accs, pieces):
+            for acc, (i, lo, hi) in zip(accs[:2], pieces[:2]):
                 p_pass(acc, a, 0, i, lo, hi)
         h0 = [sb([P, S], F32, "h0%d" % i) for i in range(4)]
-        for acc, (i, lo, hi) in zip(accs, pieces):
-            p_pass(acc, KP - 1, 0, i, lo, hi)
-            magnitude(acc, h0[i], 0, i, lo, hi)
+        sq_slots = ["sq_a", "sq_b", "slot_c", "sq_a", "sq_b"]
+        for acc, slot, (i, lo, hi) in zip(accs, sq_slots, pieces):
+            for a in range(KP - 1 if i == 0 else 0, KP):
+                p_pass(acc, a, 0, i, lo, hi)
+            magnitude(acc, h0[i], 0, i, lo, hi, slot)
             put(h0[i], i, lo, hi)
 
         for a in range(KP):
             w1_raw[a, 1] = load_w1(a, 1)
-        nc.sync.dma_start(idx3[:], offs3)
         wgt_sb = sb([P, M], F32, "wgt_sb")
         nc.sync.dma_start(out=wgt_sb[:], in_=wgt)
-        gust_sb = [sb([P, 4, M], F32, "gust%d" % b) for b in range(HP)]
+        wgt_neg = sb([P, M], F32, "wgt_neg")
+        nc.scalar.activation(wgt_neg[:], wgt_sb[:], ACT.Copy, scale=-1.0)
+        gust_sb = [sb([P, 4, M], F32, "gust%d" % b, tag="tab%d" % b) for b in range(HP)]
 
         def load_gust(b):
             nc.sync.dma_start(
@@ -180,10 +191,10 @@ def tile_list_slew_load_features_kernel(
                 in_=gust[PASS * b : PASS * (b + 1), :].rearrange("(p i) m -> p i m", i=4),
             )
 
-        load_gust(0)
         wa_raw = [load_rows(wa[PASS * b : PASS * (b + 1), :], "waraw%d" % b) for b in range(HP)]
+        load_gust(0)
         load_gust(1)
-        wd_w = sb([P, HP, N], I32, "wd_w")
+        wd_w = sb([P, HP, N], I32, "wd_w", tag="tab2")
         nc.sync.dma_start(
             out=wd_w[:], in_=wd_words.rearrange("a p c i -> p a (c i)").bitcast(I32)
         )
@@ -199,32 +210,63 @@ def tile_list_slew_load_features_kernel(
                 )
 
         for a in range(KP):
-            last = a == KP - 1
-            grouped = deal_w1(w1_raw[a, 1], "w1g%d1" % a, "x0" if last else "grp", 1 if last else 3)
+            tag, bufs = [("slot_c", 1), ("grp", 3), ("x0", 1)][a]
+            grouped = deal_w1(w1_raw[a, 1], "w1g%d1" % a, tag, bufs)
             w1_q[a, 1] = quantise(grouped, "w1q%d1" % a)
 
-        def pick(dst, i, lo, hi):
+        def pick(dst, i, lo, hi, factor):
             nc.vector.tensor_tensor(
-                dst, pages[i][:].indirect(idx3[:, lo // 16 : hi // 16]), wgt_sb[:, lo:hi], ALU.mult
+                dst, pages[i][:].indirect(idx3[:, lo // 16 : hi // 16]), factor[:, lo:hi], ALU.mult
             )
 
         x0 = sb([P, 4, M], F32, "x0", tag="x0")
         for i in range(4):
-            pick(x0[:, i, :], i, 0, M)
-        nc.vector.tensor_tensor(x0[:], x0[:], gust_sb[0][:], ALU.subtract)
+            pick(x0[:, i, :], i, 0, M, wgt_neg)
 
-        h1 = [sb([P, S], F32, "h1%d" % i, tag="slot_a" if i == 3 else None) for i in range(4)]
-        for i in range(4):
-            acc = bank((5 + i) % 8, "p1_%d" % i)
-            for a in range(KP):
-                p_pass(acc, a, 1, i, 0, S)
-            magnitude(acc, h1[i], 1, i, 0, S)
-            put(h1[i], i, 0, S)
-
-        z0 = quantise(interleave(x0, "z0g", "grp", 3), "z0")
         wa_q = [
             quantise(interleave(wa_raw[b], "wag%d" % b, "grp", 3), "waq%d" % b) for b in range(HP)
         ]
+        h1 = [sb([P, S], F32, "h1%d" % i, tag="slot_a" if i == 3 else None) for i in range(4)]
+
+        def second_half_slice(i, slot):
+            acc = bank((5 + i) % 6, "p1_%d" % i)
+            for a in range(KP):
+                p_pass(acc, a, 1, i, 0, S)
+            magnitude(acc, h1[i], 1, i, 0, S, slot)
+            put(h1[i], i, 0, S)
+
+        for i in range(3):
+            second_half_slice(i, ("sq_a", "sq_b")[i % 2])
+
+        def turn(dst, src, start, stop):
+            nc.tensor.matmul(dst, lhsT=src, rhs=ident[:], is_transpose=True, start=start, stop=stop)
+
+        def z_chunk(dst, x_neg, b, c):
+            cols = slice(CH * c, CH * (c + 1))
+            there = bank((6, 3)[c % 2], "there%d%d" % (b, c))
+            for i in range(4):
+                turn(there[:, P * i : P * (i + 1)], gust_sb[b][:, i, cols], i == 0, False)
+            for i in range(4):
+                turn(there[:, P * i : P * (i + 1)], x_neg[i], False, i == 3)
+            mid = sb([P, 4 * P], F32, "mid%d%d" % (b, c), tag=("sq_b", "sq_a")[c % 2])
+            nc.scalar.copy(out=mid[:], in_=there[:])
+            back = bank((7, 4)[c % 2], "back%d%d" % (b, c))
+            for i in range(4):
+                turn(back[:, CH * i : CH * (i + 1)], mid[:, P * i : P * (i + 1)], True, True)
+            nc.scalar.activation(
+                dst.rearrange("p (m i) -> p m i", i=4),
+                back[:].rearrange("p (i m) -> p m i", i=4),
+                ACT.Copy, scale=-1.0,
+            )
+
+        z0g = sb([P, 4 * M], BF16, "z0g", tag="grp", bufs=3)
+        for c in range(NCH):
+            z_chunk(
+                z0g[:, 4 * CH * c : 4 * CH * (c + 1)],
+                [x0[:, i, CH * c : CH * (c + 1)] for i in range(4)], 0, c,
+            )
+        z0 = quantise(z0g, "z0")
+        second_half_slice(3, "sq_a")
 
         def weights(kind, b, nt):
             cols = slice(P * nt, P * (nt + 1))
@@ -245,13 +287,23 @@ def tile_list_slew_load_features_kernel(
                     stop=(b == HP - 1 and nt == NT - 1),
                 )
 
-        y_banks = [(1, 2, 3), (4, 5, 6), (7, 0, 1), (4, 2, 3)]
+        y_banks = [(3, 4, 5), (0, 1, 2), (6, 7, 3), (0, 4, 5)]
         out_view = out.rearrange("(nt p) m -> p nt m", p=P)
+        ys = []
+
+        def finish(c):
+            y, top = ys[c]
+            best = sb([P, N], F32, "best%d" % c, tag="slot_b" if c % 2 else "slot_a")
+            nc.vector.tensor_tensor(best[:], y[1][:], top[:], ALU.max)
+            res = sb([P, NT, CH], F32, "res%d" % c, tag="res", bufs=4)
+            nc.vector.tensor_tensor(res[:].rearrange("p t m -> p (t m)"), y[2][:], best[:], ALU.add)
+            nc.sync.dma_start(out=out_view[:, :, CH * c : CH * (c + 1)], in_=res[:])
+
         for c in range(NCH):
             cols = slice(CH * c, CH * (c + 1))
             x = sb([P, 4, CH], F32, "x1%d" % c, tag="slot_b" if c % 2 else "slot_a")
             for i in range(4):
-                pick(x[:, i, :], i, CH * c, CH * (c + 1))
+                pick(x[:, i, :], i, CH * c, CH * (c + 1), wgt_sb)
             nc.vector.tensor_tensor(x[:], x[:], gust_sb[1][:, :, cols], ALU.subtract)
             z1 = quantise(interleave(x, "z1g%d" % c, "z1g", 2), "z1%d" % c)
             y = [bank(y_banks[c][kind], "y%d%d" % (kind, c)) for kind in range(3)]
@@ -259,9 +311,10 @@ def tile_list_slew_load_features_kernel(
                 y_passes(y[kind], kind, 0, z0[0][:, cols], z0[1][:, cols])
             for kind in range(3):
                 y_passes(y[kind], kind, 1, z1[0][:], z1[1][:])
-            top = sb([P, N], F32, "top%d" % c, tag="top", bufs=2)
+            top = sb([P, N], F32, "top%d" % c, tag="top", bufs=4)
             nc.scalar.activation(top[:], y[0][:], ACT.Tanh)
-            nc.vector.tensor_tensor(top[:], y[1][:], top[:], ALU.max)
-            res = sb([P, NT, CH], F32, "res%d" % c, tag="res", bufs=3)
-            nc.vector.tensor_tensor(res[:].rearrange("p t m -> p (t m)"), y[2][:], top[:], ALU.add)
-            nc.sync.dma_start(out=out_view[:, :, cols], in_=res[:])
+            ys.append((y, top))
+            if c >= 2:
+                finish(c - 2)
+        finish(2)
+        finish(3)

@@ -42,8 +42,8 @@ def tile_list_slew_load_features_kernel(
         def bank(k, name):
             return psum.tile([P, 512], F32, name=name, tag="bank%d" % k)
 
-        def load_rows(src, name):
-            raw = sb([P, 4, 512], F32, name, tag="raw", bufs=3)
+        def load_rows(src, name, slot):
+            raw = sb([P, 4, 512], F32, name, tag="raw%d" % slot)
             nc.sync.dma_start(out=raw[:], in_=src.rearrange("(p j) c -> p j c", j=4))
             return raw
 
@@ -63,17 +63,15 @@ def tile_list_slew_load_features_kernel(
             )
             return grouped
 
-        def deal_w1(raw, name, tag, bufs):
+        def deal_w1(raw, name, tag, bufs, copy):
             grouped = sb([P, 2048], BF16, name, tag=tag, bufs=bufs)
-            nc.scalar.copy(
+            copy(
                 out=grouped[:].rearrange("p (t m j) -> p m j t", t=4, j=4),
                 in_=raw[:].rearrange("p j (m t) -> p m j t", t=4),
             )
             return grouped
 
         tab_sc = sb([P, T], U8, "tab_sc")
-        wb_sc = sb([P, HP, N], U8, "wb_sc")
-        wd_sc = sb([P, HP, N], U8, "wd_sc")
         nc.gpsimd.memset(tab_sc[:].bitcast(I32), 0)
         for q in range(4):
             nc.scalar.dma_start(
@@ -86,8 +84,6 @@ def tile_list_slew_load_features_kernel(
         nc.scalar.activation(warm_out[:], warm[:], ACT.Sqrt)
         ident = sb([P, P], F32, "ident")
         make_identity(nc, ident[:])
-        nc.gpsimd.memset(wb_sc[:].bitcast(I32), 0)
-        nc.gpsimd.memset(wd_sc[:].bitcast(I32), 0)
         pages = []
         for i in range(4):
             page = sb([P, T2], F32, "page%d" % i)
@@ -111,7 +107,7 @@ def tile_list_slew_load_features_kernel(
 
         def load_w1(a, b):
             return load_rows(
-                w1[PASS * a : PASS * (a + 1), PASS * b : PASS * (b + 1)], "w1raw%d%d" % (a, b)
+                w1[PASS * a : PASS * (a + 1), PASS * b : PASS * (b + 1)], "w1raw%d%d" % (a, b), a
             )
 
         w1_raw = {}
@@ -126,7 +122,7 @@ def tile_list_slew_load_features_kernel(
 
         w1_q = {}
         for a in range(KP):
-            w1_q[a, 0] = quantise(deal_w1(w1_raw[a, 0], "w1g%d0" % a, "grp", 3), "w1q%d0" % a)
+            w1_q[a, 0] = quantise(deal_w1(w1_raw[a, 0], "w1g%d0" % a, "grp", 3, nc.vector.tensor_copy if a == 0 else nc.scalar.copy), "w1q%d0" % a)
         v_sc = sb([P, S], U8, "v_sc")
         nc.vector.tensor_copy(v_sc[:], tab_sc[:].indirect(idx[:]))
         v = [sb([P, S], U32, "v%d" % a) for a in range(KP)]
@@ -179,53 +175,56 @@ def tile_list_slew_load_features_kernel(
 
         for a in range(KP):
             w1_raw[a, 1] = load_w1(a, 1)
-        wgt_sb = sb([P, M], F32, "wgt_sb")
+        wgt_sb = sb([P, M], F32, "wgt_sb", tag="tab0")
         nc.sync.dma_start(out=wgt_sb[:], in_=wgt)
         wgt_neg = sb([P, M], F32, "wgt_neg")
         nc.scalar.activation(wgt_neg[:], wgt_sb[:], ACT.Copy, scale=-1.0)
-        gust_sb = [sb([P, 4, M], F32, "gust%d" % b, tag="tab%d" % b) for b in range(HP)]
+        gust_sb = {}
 
         def load_gust(b):
+            gust_sb[b] = sb([P, 4, M], F32, "gust%d" % b, tag="tab%d" % (b + 1))
             nc.sync.dma_start(
                 out=gust_sb[b][:],
                 in_=gust[PASS * b : PASS * (b + 1), :].rearrange("(p i) m -> p i m", i=4),
             )
 
-        wa_raw = [load_rows(wa[PASS * b : PASS * (b + 1), :], "waraw%d" % b) for b in range(HP)]
         load_gust(0)
         load_gust(1)
-        wd_w = sb([P, HP, N], I32, "wd_w", tag="tab2")
-        nc.sync.dma_start(
-            out=wd_w[:], in_=wd_words.rearrange("a p c i -> p a (c i)").bitcast(I32)
-        )
-        wb_w = sb([P, HP, 2 * N], U8, "wb_w")
+        wb_w = sb([P, HP, 2 * N], U8, "wb_w", tag="h00")
         nc.sync.dma_start(
             out=wb_w[:].bitcast(I32), in_=wb_words.rearrange("a p c -> p a c").bitcast(I32)
         )
-        for plane, src in ((wd_sc, wd_scales), (wb_sc, wb_scales)):
+
+        for a in range(KP):
+            tag, bufs = [("slot_c", 1), ("x0_0", 1), ("x0_1", 1)][a]
+            grouped = deal_w1(w1_raw[a, 1], "w1g%d1" % a, tag, bufs, nc.scalar.copy)
+            w1_q[a, 1] = quantise(grouped, "w1q%d1" % a)
+
+        wa_raw = [load_rows(wa[PASS * b : PASS * (b + 1), :], "waraw%d" % b, b) for b in range(HP)]
+        wd_w = sb([P, HP, N], I32, "wd_w", tag="slot_c")
+        nc.sync.dma_start(
+            out=wd_w[:], in_=wd_words.rearrange("a p c i -> p a (c i)").bitcast(I32)
+        )
+        planes = sb([P, 2, HP, N], U8, "planes", tag="raw2")
+        wb_sc, wd_sc = planes[:, 0], planes[:, 1]
+        nc.gpsimd.memset(planes[:].rearrange("p k a c -> p (k a c)").bitcast(I32), 0)
+        for plane, src in ((wb_sc, wb_scales), (wd_sc, wd_scales)):
             for q in range(4):
                 nc.sync.dma_start(
                     out=plane[32 * q : 32 * q + 4, :, :].bitcast(I32),
                     in_=src[:, 4 * q : 4 * q + 4, :].rearrange("a r c -> r a c").bitcast(I32),
                 )
 
-        for a in range(KP):
-            tag, bufs = [("slot_c", 1), ("grp", 3), ("x0", 1)][a]
-            grouped = deal_w1(w1_raw[a, 1], "w1g%d1" % a, tag, bufs)
-            w1_q[a, 1] = quantise(grouped, "w1q%d1" % a)
-
         def pick(dst, i, lo, hi, factor):
             nc.vector.tensor_tensor(
                 dst, pages[i][:].indirect(idx3[:, lo // 16 : hi // 16]), factor[:, lo:hi], ALU.mult
             )
 
-        x0 = sb([P, 4, M], F32, "x0", tag="x0")
+        x0 = [sb([P, 2, M], F32, "x0_%d" % k) for k in range(2)]
         for i in range(4):
-            pick(x0[:, i, :], i, 0, M, wgt_neg)
+            pick(x0[i // 2][:, i % 2, :], i, 0, M, wgt_neg)
 
-        wa_q = [
-            quantise(interleave(wa_raw[b], "wag%d" % b, "grp", 3), "waq%d" % b) for b in range(HP)
-        ]
+        wa_q = [quantise(interleave(wa_raw[0], "wag0", "grp", 3), "waq0")]
         h1 = [sb([P, S], F32, "h1%d" % i, tag="slot_a" if i == 3 else None) for i in range(4)]
 
         def second_half_slice(i, slot):
@@ -236,21 +235,24 @@ def tile_list_slew_load_features_kernel(
             put(h1[i], i, 0, S)
 
         for i in range(3):
-            second_half_slice(i, ("sq_a", "sq_b")[i % 2])
+            second_half_slice(i, "raw0")
+
 
         def turn(dst, src, start, stop):
             nc.tensor.matmul(dst, lhsT=src, rhs=ident[:], is_transpose=True, start=start, stop=stop)
 
+        mids = sb([P, NCH, 4 * P], F32, "mids", tag="raw0")
+
         def z_chunk(dst, x_neg, b, c):
             cols = slice(CH * c, CH * (c + 1))
-            there = bank((6, 3)[c % 2], "there%d%d" % (b, c))
+            there = bank((3, 4, 6, 7)[c], "there%d%d" % (b, c))
             for i in range(4):
                 turn(there[:, P * i : P * (i + 1)], gust_sb[b][:, i, cols], i == 0, False)
             for i in range(4):
                 turn(there[:, P * i : P * (i + 1)], x_neg[i], False, i == 3)
-            mid = sb([P, 4 * P], F32, "mid%d%d" % (b, c), tag=("sq_b", "sq_a")[c % 2])
-            nc.scalar.copy(out=mid[:], in_=there[:])
-            back = bank((7, 4)[c % 2], "back%d%d" % (b, c))
+            mid = mids[:, c, :]
+            nc.scalar.copy(out=mid, in_=there[:])
+            back = bank((5, 0, 1)[c % 3], "back%d%d" % (b, c))
             for i in range(4):
                 turn(back[:, CH * i : CH * (i + 1)], mid[:, P * i : P * (i + 1)], True, True)
             nc.scalar.activation(
@@ -263,10 +265,11 @@ def tile_list_slew_load_features_kernel(
         for c in range(NCH):
             z_chunk(
                 z0g[:, 4 * CH * c : 4 * CH * (c + 1)],
-                [x0[:, i, CH * c : CH * (c + 1)] for i in range(4)], 0, c,
+                [x0[i // 2][:, i % 2, CH * c : CH * (c + 1)] for i in range(4)], 0, c,
             )
         z0 = quantise(z0g, "z0")
-        second_half_slice(3, "sq_a")
+        second_half_slice(3, "raw0")
+        wa_q.append(quantise(interleave(wa_raw[1], "wag1", "raw0", 1), "waq1"))
 
         def weights(kind, b, nt):
             cols = slice(P * nt, P * (nt + 1))
@@ -287,7 +290,7 @@ def tile_list_slew_load_features_kernel(
                     stop=(b == HP - 1 and nt == NT - 1),
                 )
 
-        y_banks = [(3, 4, 5), (0, 1, 2), (6, 7, 3), (0, 4, 5)]
+        y_banks = [(3, 4, 6), (7, 0, 1), (5, 2, 3), (7, 4, 6)]
         out_view = out.rearrange("(nt p) m -> p nt m", p=P)
         ys = []
 
@@ -301,7 +304,7 @@ def tile_list_slew_load_features_kernel(
 
         for c in range(NCH):
             cols = slice(CH * c, CH * (c + 1))
-            x = sb([P, 4, CH], F32, "x1%d" % c, tag="slot_b" if c % 2 else "slot_a")
+            x = sb([P, 4, CH], F32, "x1%d" % c, tag=("h12", "h11", "slot_a", "slot_b")[c])
             for i in range(4):
                 pick(x[:, i, :], i, CH * c, CH * (c + 1), wgt_sb)
             nc.vector.tensor_tensor(x[:], x[:], gust_sb[1][:, :, cols], ALU.subtract)

from contextlib import ExitStack

import concourse.mybir as mybir
from concourse.masks import make_identity

K, T, S, H, T2, M, N = 1536, 2048, 512, 1024, 1024, 512, 512
FLOPS = 2 * K * H * S + 3 * 2 * H * N * M

F32 = mybir.dt.float32
BF16 = mybir.dt.bfloat16
I32 = mybir.dt.int32
U32 = mybir.dt.uint32
U16 = mybir.dt.uint16
U8 = mybir.dt.uint8
FP8X4 = mybir.dt.float8_e4m3fn_x4
FP4X4 = mybir.dt.float4_e2m1fn_x4
ACT = mybir.ActivationFunctionType
ALU = mybir.AluOpType

P = 128
PASS = 512
KP = K // PASS
HP = H // PASS
CH = 128
NCH = M // CH
NT = N // P


def tile_list_slew_load_features_kernel(
    tc, tab_words, tab_scales, offs, w1, unit, offs2, wgs, offs3, wgt, gust, wa,
    wb_words, wb_scales, wd_words, wd_scales, out,
):
    nc = tc.nc
    with ExitStack() as ctx:
        lists = ctx.enter_context(tc.tile_pool(name="lists", bufs=1))
        keep = ctx.enter_context(tc.tile_pool(name="keep", bufs=1))
        psum = ctx.enter_context(tc.psum_pool(name="psum", bufs=1))

        def sb(shape, dtype, name, tag=None, bufs=1):
            return keep.tile(shape, dtype, name=name, tag=tag or name, bufs=bufs, align_bytes=64)

        def bank(k, name):
            return psum.tile([P, 512], F32, name=name, tag="bank%d" % k)

        def load_rows(src, name, slot):
            raw = sb([P, 4, 512], F32, name, tag="raw%d" % slot)
            nc.sync.dma_start(out=raw[:], in_=src.rearrange("(p j) c -> p j c", j=4))
            return raw

        def quantise(grouped, name):
            width = grouped.shape[1] // 4
            codes = sb([P, width], U32, name + "_codes")
            scales = sb([P, width], U8, name + "_scales")
            nc.vector.quantize_mx(out=codes[:].bitcast(FP8X4), scales=scales[:], in_=grouped[:])
            return codes, scales

        def interleave(src, name, tag, bufs):
            width = src.shape[2]
            grouped = sb([P, 4 * width], BF16, name, tag=tag, bufs=bufs)
            nc.scalar.copy(
                out=grouped[:].rearrange("p (a c j) -> p a j c", c=4, j=4),
                in_=src[:].rearrange("p j (a c) -> p a j c", c=4),
            )
            return grouped

        def deal_w1(raw, name, tag, bufs, copy):
            grouped = sb([P, 2048], BF16, name, tag=tag, bufs=bufs)
            copy(
                out=grouped[:].rearrange("p (t m j) -> p m j t", t=4, j=4),
                in_=raw[:].rearrange("p j (m t) -> p m j t", t=4),
            )
            return grouped

        tab_sc = sb([P, T], U8, "tab_sc")
        nc.gpsimd.memset(tab_sc[:].bitcast(I32), 0)
        for q in range(4):
            nc.scalar.dma_start(
                out=tab_sc[32 * q : 32 * q + 4 * KP, :].bitcast(I32),
                in_=tab_scales[:, 4 * q : 4 * q + 4, :].bitcast(I32),
            )
        warm = sb([P, 8], F32, "warm")
        nc.gpsimd.memset(warm[:], 1.0)
        warm_out = sb([P, 8], F32, "warm_out")
        nc.scalar.activation(warm_out[:], warm[:], ACT.Sqrt)
        ident = sb([P, P], F32, "ident")
        make_identity(nc, ident[:])
        pages = []
        for i in range(4):
            page = sb([P, T2], F32, "page%d" % i)
            nc.vector.memset(page[:], 0.0)
            pages.append(page)

        idx = lists.tile([P, S // 16], U16, name="idx")
        idx2 = lists.tile([P, S // 16], U16, name="idx2")
        idx3 = lists.tile([P, M // 16], U16, name="idx3")
        nc.sync.dma_start(idx[:], offs)
        nc.sync.dma_start(idx2[:], offs2)
        nc.sync.dma_start(idx3[:], offs3)
        unit_sb = sb([P, HP, 4], F32, "unit_sb")
        nc.sync.dma_start(out=unit_sb[:], in_=unit.rearrange("(b p i) -> p b i", b=HP, i=4))
        tab = [sb([P, T], I32, "tab%d" % a) for a in range(KP)]

        def load_tab(a):
            nc.sync.dma_start(
                out=tab[a][:], in_=tab_words[a].rearrange("p t i -> p (t i)").bitcast(I32)
            )

        def load_w1(a, b):
            return load_rows(
                w1[PASS * a : PASS * (a + 1), PASS * b : PASS * (b + 1)], "w1raw%d%d" % (a, b), a
            )

        w1_raw = {}
        w1_raw[0, 0] = load_w1(0, 0)
        w1_raw[1, 0] = load_w1(1, 0)
        load_tab(0)
        w1_raw[2, 0] = load_w1(2, 0)
        load_tab(1)
        load_tab(2)
        wgs_sb = sb([P, S], F32, "wgs_sb", tag="slot_b")
        nc.sync.dma_start(out=wgs_sb[:], in_=wgs)

        w1_q = {}
        for a in range(KP):
            w1_q[a, 0] = quantise(deal_w1(w1_raw[a, 0], "w1g%d0" % a, "grp", 3, nc.vector.tensor_copy if a == 0 else nc.scalar.copy), "w1q%d0" % a)
        v_sc = sb([P, S], U8, "v_sc")
        nc.vector.tensor_copy(v_sc[:], tab_sc[:].indirect(idx[:]))
        v = [sb([P, S], U32, "v%d" % a) for a in range(KP)]
        for a in range(KP - 1):
            nc.vector.tensor_copy(v[a][:], tab[a][:].bitcast(U32).indirect(idx[:]))
        half = S // 2
        for lo in (0, half):
            nc.vector.tensor_copy(
                v[KP - 1][:, lo : lo + half],
                tab[KP - 1][:].bitcast(U32).indirect(idx[:, lo // 16 : (lo + half) // 16]),
            )

        def p_pass(acc, a, b, i, lo, hi):
            codes, scales = w1_q[a, b]
            nc.tensor.matmul_mx(
                out=acc[:, 0 : hi - lo],
                lhsT=codes[:, P * i : P * (i + 1)].bitcast(FP8X4),
                lhsT_scale=scales[:, P * i : P * (i + 1)],
                rhs=v[a][:, lo:hi].bitcast(FP8X4),
                rhs_scale=v_sc[4 * a : P, lo:hi],
                start=(a == 0),
                stop=(a == KP - 1),
            )

        def magnitude(acc, h, b, i, lo, hi, slot):
            sq = sb([P, S], F32, "sq%d%d%d" % (b, i, lo), tag=slot)
            nc.scalar.activation(sq[:, 0 : hi - lo], acc[:, 0 : hi - lo], ACT.Square)
            nc.scalar.activation(
                h[:, lo:hi], sq[:, 0 : hi - lo], ACT.Sqrt, bias=unit_sb[:, b, i : i + 1]
            )

        def put(h, i, lo, hi):
            nc.vector.tensor_tensor(
                pages[i][:].indirect(idx2[:, lo // 16 : hi // 16]),
                h[:, lo:hi], wgs_sb[:, lo:hi], ALU.mult,
            )

        pieces = [(0, 0, half), (0, half, S), (1, 0, S), (2, 0, S), (3, 0, S)]
        accs = [bank(k, "p0_%d" % k) for k in range(len(pieces))]
        for a in range(KP - 1):
            for acc, (i, lo, hi) in zip(accs[:2], pieces[:2]):
                p_pass(acc, a, 0, i, lo, hi)
        h0 = [sb([P, S], F32, "h0%d" % i) for i in range(4)]
        sq_slots = ["sq_a", "sq_b", "slot_c", "sq_a", "sq_b"]
        for acc, slot, (i, lo, hi) in zip(accs, sq_slots, pieces):
            for a in range(KP - 1 if i == 0 else 0, KP):
                p_pass(acc, a, 0, i, lo, hi)
            magnitude(acc, h0[i], 0, i, lo, hi, slot)
            put(h0[i], i, lo, hi)

        for a in range(KP):
            w1_raw[a, 1] = load_w1(a, 1)
        wgt_sb = sb([P, M], F32, "wgt_sb", tag="tab0")
        nc.sync.dma_start(out=wgt_sb[:], in_=wgt)
        wgt_neg = sb([P, M], F32, "wgt_neg")
        nc.scalar.activation(wgt_neg[:], wgt_sb[:], ACT.Copy, scale=-1.0)
        gust_sb = {}

        def load_gust(b):
            gust_sb[b] = sb([P, 4, M], F32, "gust%d" % b, tag="tab%d" % (b + 1))
            nc.sync.dma_start(
                out=gust_sb[b][:],
                in_=gust[PASS * b : PASS * (b + 1), :].rearrange("(p i) m -> p i m", i=4),
            )

        load_gust(0)
        load_gust(1)
        wb_w = sb([P, HP, 2 * N], U8, "wb_w", tag="h00")
        nc.sync.dma_start(
            out=wb_w[:].bitcast(I32), in_=wb_words.rearrange("a p c -> p a c").bitcast(I32)
        )

        for a in range(KP):
            tag, bufs = [("slot_c", 1), ("x0_0", 1), ("x0_1", 1)][a]
            grouped = deal_w1(w1_raw[a, 1], "w1g%d1" % a, tag, bufs, nc.scalar.copy)
            w1_q[a, 1] = quantise(grouped, "w1q%d1" % a)

        wa_raw = [load_rows(wa[PASS * b : PASS * (b + 1), :], "waraw%d" % b, b) for b in range(HP)]
        wd_w = sb([P, HP, N], I32, "wd_w", tag="slot_c")
        nc.sync.dma_start(
            out=wd_w[:], in_=wd_words.rearrange("a p c i -> p a (c i)").bitcast(I32)
        )
        planes = sb([P, 2, HP, N], U8, "planes", tag="raw2")
        wb_sc, wd_sc = planes[:, 0], planes[:, 1]
        nc.gpsimd.memset(planes[:].rearrange("p k a c -> p (k a c)").bitcast(I32), 0)
        for plane, src in ((wb_sc, wb_scales), (wd_sc, wd_scales)):
            for q in range(4):
                nc.sync.dma_start(
                    out=plane[32 * q : 32 * q + 4, :, :].bitcast(I32),
                    in_=src[:, 4 * q : 4 * q + 4, :].rearrange("a r c -> r a c").bitcast(I32),
                )

        def pick(dst, i, lo, hi, factor):
            nc.vector.tensor_tensor(
                dst, pages[i][:].indirect(idx3[:, lo // 16 : hi // 16]), factor[:, lo:hi], ALU.mult
            )

        x0 = [sb([P, 2, M], F32, "x0_%d" % k) for k in range(2)]
        for i in range(4):
            pick(x0[i // 2][:, i % 2, :], i, 0, M, wgt_neg)

        wa_q = [quantise(interleave(wa_raw[0], "wag0", "grp", 3), "waq0")]
        h1 = [sb([P, S], F32, "h1%d" % i, tag="slot_a" if i == 3 else None) for i in range(4)]

        def second_half_slice(i, slot):
            acc = bank((5 + i) % 6, "p1_%d" % i)
            for a in range(KP):
                p_pass(acc, a, 1, i, 0, S)
            magnitude(acc, h1[i], 1, i, 0, S, slot)
            put(h1[i], i, 0, S)

        for i in range(3):
            second_half_slice(i, "raw0")


        def turn(dst, src, start, stop):
            nc.tensor.matmul(dst, lhsT=src, rhs=ident[:], is_transpose=True, start=start, stop=stop)

        mids = sb([P, NCH, 4 * P], F32, "mids", tag="raw0")

        def z_chunk(dst, x_neg, b, c):
            cols = slice(CH * c, CH * (c + 1))
            there = bank((3, 4, 6, 7)[c], "there%d%d" % (b, c))
            for i in range(4):
                turn(there[:, P * i : P * (i + 1)], gust_sb[b][:, i, cols], i == 0, False)
            for i in range(4):
                turn(there[:, P * i : P * (i + 1)], x_neg[i], False, i == 3)
            mid = mids[:, c, :]
            nc.scalar.copy(out=mid, in_=there[:])
            back = bank((5, 0, 1)[c % 3], "back%d%d" % (b, c))
            for i in range(4):
                turn(back[:, CH * i : CH * (i + 1)], mid[:, P * i : P * (i + 1)], True, True)
            nc.scalar.activation(
                dst.rearrange("p (m i) -> p m i", i=4),
                back[:].rearrange("p (i m) -> p m i", i=4),
                ACT.Copy, scale=-1.0,
            )

        z0g = sb([P, 4 * M], BF16, "z0g", tag="grp", bufs=3)
        for c in range(NCH):
            z_chunk(
                z0g[:, 4 * CH * c : 4 * CH * (c + 1)],
                [x0[i // 2][:, i % 2, CH * c : CH * (c + 1)] for i in range(4)], 0, c,
            )
        z0 = quantise(z0g, "z0")
        second_half_slice(3, "raw0")
        wa_q.append(quantise(interleave(wa_raw[1], "wag1", "raw0", 1), "waq1"))

        def weights(kind, b, nt):
            cols = slice(P * nt, P * (nt + 1))
            if kind == 0:
                return wa_q[b][0][:, cols].bitcast(FP8X4), wa_q[b][1][:, cols]
            if kind == 1:
                return wb_w[:, b, 2 * P * nt : 2 * P * (nt + 1)].bitcast(FP4X4), wb_sc[:, b, cols]
            return wd_w[:, b, cols].bitcast(FP8X4), wd_sc[:, b, cols]

        def y_passes(acc, kind, b, z_codes, z_scales):
            for nt in range(NT):
                w_codes, w_scales = weights(kind, b, nt)
                nc.tensor.matmul_mx(
                    out=acc[:, CH * nt : CH * (nt + 1)],
                    lhsT=w_codes, lhsT_scale=w_scales,
                    rhs=z_codes.bitcast(FP8X4), rhs_scale=z_scales,
                    start=(b == 0 and nt == 0),
                    stop=(b == HP - 1 and nt == NT - 1),
                )

        y_banks = [(3, 4, 6), (7, 0, 1), (5, 2, 3), (7, 4, 6)]
        out_view = out.rearrange("(nt p) m -> p nt m", p=P)
        ys = []

        def finish(c):
            y, top = ys[c]
            best = sb([P, N], F32, "best%d" % c, tag="slot_b" if c % 2 else "slot_a")
            nc.vector.tensor_tensor(best[:], y[1][:], top[:], ALU.max)
            res = sb([P, NT, CH], F32, "res%d" % c, tag="res", bufs=4)
            nc.vector.tensor_tensor(res[:].rearrange("p t m -> p (t m)"), y[2][:], best[:], ALU.add)
            nc.sync.dma_start(out=out_view[:, :, CH * c : CH * (c + 1)], in_=res[:])

        for c in range(NCH):
            cols = slice(CH * c, CH * (c + 1))
            x = sb([P, 4, CH], F32, "x1%d" % c, tag=("h12", "h11", "slot_a", "slot_b")[c])
            for i in range(4):
                pick(x[:, i, :], i, CH * c, CH * (c + 1), wgt_sb)
            nc.vector.tensor_tensor(x[:], x[:], gust_sb[1][:, :, cols], ALU.subtract)
            z1 = quantise(interleave(x, "z1g%d" % c, "z1g", 2), "z1%d" % c)
            y = [bank(y_banks[c][kind], "y%d%d" % (kind, c)) for kind in range(3)]
            for kind in range(3):
                y_passes(y[kind], kind, 0, z0[0][:, cols], z0[1][:, cols])
            for kind in range(3):
                y_passes(y[kind], kind, 1, z1[0][:], z1[1][:])
            top = sb([P, N], F32, "top%d" % c, tag="top", bufs=4)
            nc.scalar.activation(top[:], y[0][:], ACT.Tanh)
            ys.append((y, top))
            if c >= 2:
                finish(c - 2)
        finish(2)
        finish(3)
